import numpy as np
import ml_dtypes


def mxq(x, axis, fmt="e4m3"):
    dtype, down = {"e4m3": (ml_dtypes.float8_e4m3fn, 7), "e5m2": (ml_dtypes.float8_e5m2, 14)}[fmt]
    v = np.moveaxis(np.asarray(x, np.float32).astype(ml_dtypes.bfloat16).astype(np.float64), axis, -1)
    blocks = v.reshape(v.shape[:-1] + (-1, 32))
    amax = np.abs(blocks).max(-1, keepdims=True)
    byte = np.maximum(np.where(amax > 0, np.frexp(amax)[1] - 1 + 127, 0) - down, 1)
    scale = np.exp2(byte - 127.0)
    codes = (blocks / scale).astype(np.float32).astype(dtype).astype(np.float64)
    return np.moveaxis((codes * scale).reshape(v.shape), -1, axis)


WIDE = False


def mx_kscale(k, group=512):
    if not WIDE:
        return np.ones(k)
    levels = np.array([10, -10, 5, -5, 0])
    if group != 512:
        return np.exp2(np.random.permutation(np.resize(levels, k // group))).repeat(group)
    if k % 512:
        return np.exp2(np.random.permutation(np.resize(levels, k // 32))).repeat(32)
    a = np.empty((k // 512, 16))
    for p in range(k // 512):
        a[p, :8] = np.random.permutation(np.resize(levels, 8))
        for g in range(8):
            far = levels[np.abs(levels - a[p, g]) >= 10]
            a[p, g + 8] = far[np.random.randint(len(far))]
    return np.exp2(a.ravel()).repeat(32)


def f64(x):
    return np.asarray(x).astype(np.float64)


def sigmoid(v):
    return 1.0 / (1.0 + np.exp(-v))


G, D, M, O, N = 2, 256, 128, 256, 512


def setup_inputs():
    n = np.random.standard_normal
    s_d = mx_kscale(D, 0)
    s_o = mx_kscale(O, 0)
    return {
        "x": (n((G, D, N)) * s_d[:, None]).astype(np.float32),
        "w1": (n((G, D, M)) / np.sqrt(D) / s_d[:, None]).astype(np.float32),
        "w2": (n((G, D, M)) / np.sqrt(D) / s_d[:, None]).astype(np.float32),
        "w3": (n((G, D, M)) / np.sqrt(D) / s_d[:, None]).astype(np.float32),
        "th": (0.5 * n((G, M, 1))).astype(np.float32),
        "wo": (n((G, O, M)) / np.sqrt(O) / s_o[:, None]).astype(np.float32),
        "dy": (n((G, O, N)) * s_o[:, None]).astype(np.float32),
        "og": (np.random.uniform(0.3, 1.0, (G, M, 1))).astype(np.float32),
        "base": (0.2 * n((G, M, N))).astype(np.float32),
    }


def reference(x, w1, w2, w3, th, wo, dy, og, base):
    w1q = mxq(f64(w1), 1, "e4m3")
    xq = mxq(f64(x), 1, "e4m3")
    z1 = w1q.transpose(0, 2, 1) @ xq
    w2q = mxq(f64(w2), 1, "e4m3")
    z2 = w2q.transpose(0, 2, 1) @ xq
    w3q = mxq(f64(w3), 1, "e4m3")
    z3 = w3q.transpose(0, 2, 1) @ xq
    g2 = sigmoid(z2)
    g3 = sigmoid(z3 - f64(th))
    woq = mxq(f64(wo), 1, "e4m3")
    dyq = mxq(f64(dy), 1, "e4m3")
    c0 = woq.transpose(0, 2, 1) @ dyq
    dg2 = c0 * g3 * z1
    dz2 = dg2 * g2 * (1.0 - g2)
    kdz2 = dz2 * 2.0
    kg2 = kdz2 * (1.0 - g2) * dg2 - kdz2 * dg2 * g2
    kz2 = kg2 * g2 * (1.0 - g2)
    y = kz2 * f64(og) + f64(base)
    return y

@@ -1,0 +1,194 @@
+from contextlib import ExitStack
+
+import concourse.mybir as mybir
+
+G, D, M, N = 2, 256, 128, 512
+FLOPS = 4 * 2 * G * D * M * N
+
+F32 = mybir.dt.float32
+BF16 = mybir.dt.bfloat16
+U32 = mybir.dt.uint32
+U8 = mybir.dt.uint8
+FP8X4 = mybir.dt.float8_e4m3fn_x4
+ACT = mybir.ActivationFunctionType
+ALU = mybir.AluOpType
+
+P = 128
+PACK = 4
+ROWS = 64
+HALF = N // 2
+NMM = 128
+RUN = 4
+
+
+def tile_rows_gptwogates_kernel(tc, x, w1, w2, w3, th, wo, dy, og, base, out):
+    nc = tc.nc
+    with ExitStack() as ctx:
+        sb = ctx.enter_context(tc.tile_pool(name="sb", bufs=1))
+        ps = ctx.enter_context(tc.psum_pool(name="ps", bufs=1))
+
+        def load(name, src, c0, width):
+            raw = sb.tile([P, PACK, width], F32, name="raw_" + name, align_bytes=64)
+            nc.sync.dma_start(out=raw[:], in_=src.rearrange("g (p j) c -> (g p) j c", j=PACK)[:, :, c0 : c0 + width])
+            return raw
+
+        raw = {}
+        raw["w3"] = load("w3", w3, 0, M)
+        raw["x0"] = load("x0", x, 0, HALF)
+        raw["w1"] = load("w1", w1, 0, M)
+        raw["w2"] = load("w2", w2, 0, M)
+        raw["x1"] = load("x1", x, HALF, HALF)
+        raw["wo"] = load("wo", wo, 0, M)
+        raw["dy0"] = load("dy0", dy, 0, HALF)
+        raw["dy1"] = load("dy1", dy, HALF, HALF)
+        base_sb = sb.tile([P, G, N], F32, name="base_sb")
+        nc.sync.dma_start(out=base_sb[:], in_=base.rearrange("g m n -> m g n"))
+
+        th_sb = sb.tile([P, G, 8], F32, name="th_sb")
+        og_sb = sb.tile([P, G, 8], F32, name="og_sb")
+        with nc.allow_non_contiguous_dma(reason="one value a partition"):
+            nc.gpsimd.dma_start(out=th_sb[:, :, 0:1], in_=th.rearrange("g m o -> m g o"))
+            nc.gpsimd.dma_start(out=og_sb[:, :, 0:1], in_=og.rearrange("g m o -> m g o"))
+        bias3 = sb.tile([P, G, 8], F32, name="bias3")
+        nc.gpsimd.tensor_scalar(out=bias3[:, :, 0:1], in0=th_sb[:, :, 0:1], scalar1=-0.5, scalar2=0.0, op0=ALU.mult, op1=ALU.add)
+
+        words = {}
+        for name in raw:
+            words[name] = sb.tile([P, raw[name].shape[2], PACK], BF16, name="bf_" + name, align_bytes=64)
+
+        def interleave(copy, name, c0, c1):
+            copy(
+                out=words[name][:, c0:c1, :].rearrange("p (c i) j -> p c j i", i=RUN),
+                in_=raw[name][:, :, c0:c1].rearrange("p j (c i) -> p c j i", i=RUN),
+            )
+
+        codes, scales = {}, {}
+
+        def quantize(name):
+            width = raw[name].shape[2]
+            codes[name] = sb.tile([P, width], U32, name="codes_" + name, align_bytes=64)
+            scales[name] = sb.tile([P, width], U8, name="scales_" + name, align_bytes=64)
+            nc.vector.quantize_mx(
+                out=codes[name][:].bitcast(FP8X4),
+                scales=scales[name][:],
+                in_=words[name][:].rearrange("p c j -> p (c j)"),
+            )
+
+        banks = {}
+        for z in ("z1", "z2", "z3", "c0"):
+            for g in range(G):
+                banks[z, g] = ps.tile([M, N], F32, name="%s_%d" % (z, g))
+
+        def product(z, weight, moving, h):
+            for c in range(0, HALF, NMM):
+                for g in range(G):
+                    rows = slice(ROWS * g, ROWS * (g + 1))
+                    nc.tensor.matmul_mx(
+                        out=banks[z, g][:, h * HALF + c : h * HALF + c + NMM],
+                        lhsT=codes[weight][rows, :].bitcast(FP8X4),
+                        lhsT_scale=scales[weight][rows, :],
+                        rhs=codes[moving][rows, c : c + NMM].bitcast(FP8X4),
+                        rhs_scale=scales[moving][rows, c : c + NMM],
+                        start=True,
+                        stop=True,
+                    )
+
+        work = {}
+        for name in ("t3", "t2", "t2sq", "p", "v", "w", "wsq", "m", "y"):
+            for h in range(2):
+                work[name, h] = sb.tile([P, G, HALF], F32, name="%s_%d" % (name, h))
+
+        def psum(z, g, h):
+            return banks[z, g][:, h * HALF : (h + 1) * HALF]
+
+        def tanh3(h, g):
+            nc.scalar.activation(out=work["t3", h][:, g, :], in_=psum("z3", g, h), func=ACT.Tanh, bias=bias3[:, g, 0:1], scale=0.5)
+
+        def tanh2(h, g):
+            nc.scalar.activation(out=work["t2", h][:, g, :], in_=psum("z2", g, h), func=ACT.Tanh, scale=0.5)
+
+        def sq2(h):
+            nc.scalar.activation(out=work["t2sq", h][:], in_=work["t2", h][:], func=ACT.Square)
+
+        def step_p(h, g):
+            nc.vector.scalar_tensor_tensor(out=work["p", h][:, g, :], in0=work["t3", h][:, g, :], scalar=1.0, in1=psum("z1", g, h), op0=ALU.add, op1=ALU.mult)
+
+        def step_v(h):
+            nc.vector.scalar_tensor_tensor(out=work["v", h][:], in0=work["t2sq", h][:], scalar=1.0, in1=work["p", h][:], op0=ALU.subtract, op1=ALU.mult)
+
+        def step_w(h, g):
+            nc.vector.tensor_tensor(out=work["w", h][:, g, :], in0=work["v", h][:, g, :], in1=psum("c0", g, h), op=ALU.mult)
+
+        def sqw(h, gs):
+            nc.scalar.activation(out=work["wsq", h][:, gs, :], in_=work["w", h][:, gs, :], func=ACT.Square)
+
+        def step_m(h, gs):
+            nc.vector.scalar_tensor_tensor(out=work["m", h][:, gs, :], in0=work["wsq", h][:, gs, :], scalar=-1.0 / 32.0, in1=work["t2", h][:, gs, :], op0=ALU.mult, op1=ALU.mult)
+
+        def step_y(h, g):
+            nc.vector.scalar_tensor_tensor(out=work["y", h][:, g, :], in0=work["m", h][:, g, :], scalar=og_sb[:, g, 0:1], in1=base_sb[:, g, h * HALF : (h + 1) * HALF], op0=ALU.mult, op1=ALU.add)
+
+        def store(h, gs):
+            nc.sync.dma_start(out=out.rearrange("g m n -> m g n")[:, gs, h * HALF : (h + 1) * HALF], in_=work["y", h][:, gs, :])
+
+        vec, act = nc.vector.tensor_copy, nc.scalar.copy
+        both = slice(0, G)
+        with tc.manual_schedule():
+            interleave(vec, "w3", 0, M)
+            quantize("w3")
+            interleave(vec, "x0", 0, 160)
+            interleave(act, "x0", 160, HALF)
+            quantize("x0")
+            product("z3", "w3", "x0", 0)
+            interleave(act, "w1", 0, M)
+            interleave(vec, "w2", 0, M)
+            quantize("w1")
+            product("z1", "w1", "x0", 0)
+            quantize("w2")
+            product("z2", "w2", "x0", 0)
+            tanh3(0, 0)
+            tanh3(0, 1)
+            step_p(0, 0)
+            interleave(vec, "x1", 0, HALF)
+            step_p(0, 1)
+            tanh2(0, 0)
+            tanh2(0, 1)
+            quantize("x1")
+            product("z3", "w3", "x1", 1)
+            product("z2", "w2", "x1", 1)
+            product("z1", "w1", "x1", 1)
+            interleave(act, "wo", 0, M)
+            sq2(0)
+            quantize("wo")
+            interleave(vec, "dy0", 0, HALF)
+            step_v(0)
+            quantize("dy0")
+            product("c0", "wo", "dy0", 0)
+            tanh3(1, 0)
+            tanh3(1, 1)
+            tanh2(1, 0)
+            tanh2(1, 1)
+            step_p(1, 0)
+            step_p(1, 1)
+            interleave(act, "dy1", 0, HALF)
+            step_w(0, 0)
+            step_w(0, 1)
+            quantize("dy1")
+            product("c0", "wo", "dy1", 1)
+            sq2(1)
+            sqw(0, both)
+            step_v(1)
+            step_m(0, both)
+            step_w(1, 0)
+            step_w(1, 1)
+            sqw(1, slice(0, 1))
+            sqw(1, slice(1, 2))
+            step_y(0, 0)
+            step_y(0, 1)
+            store(0, both)
+            step_m(1, slice(0, 1))
+            step_m(1, slice(1, 2))
+            step_y(1, 0)
+            store(1, slice(0, 1))
+            step_y(1, 1)
+            store(1, slice(1, 2))

@@ -15,10 +15,13 @@ ALU = mybir.AluOpType
 
 P = 128
 PACK = 4
-ROWS = 64
+ROWS = D // PACK
 HALF = N // 2
-NMM = 128
+N_MM = 128
 RUN = 4
+QUAD = 32
+X0_VECTOR = 168
+X1_VECTOR = 128
 
 
 def tile_rows_gptwogates_kernel(tc, x, w1, w2, w3, th, wo, dy, og, base, out):
@@ -26,52 +29,56 @@ def tile_rows_gptwogates_kernel(tc, x, w1, w2, w3, th, wo, dy, og, base, out):
     with ExitStack() as ctx:
         sb = ctx.enter_context(tc.tile_pool(name="sb", bufs=1))
         ps = ctx.enter_context(tc.psum_pool(name="ps", bufs=1))
+        ctx.enter_context(tc.manual_schedule())
 
-        def load(name, src, c0, width):
-            raw = sb.tile([P, PACK, width], F32, name="raw_" + name, align_bytes=64)
-            nc.sync.dma_start(out=raw[:], in_=src.rearrange("g (p j) c -> (g p) j c", j=PACK)[:, :, c0 : c0 + width])
-            return raw
+        vec_rows = sb.tile([P, 2 * G, QUAD], F32, name="vec_rows", align_bytes=64)
+        nc.vector.memset(vec_rows[:], 0.0)
+        zero = sb.tile([P, G, 1], F32, name="zero")
+        nc.vector.memset(zero[:], 0.0)
+        one_half = sb.tile([P, G, 1], F32, name="one_half")
+        nc.scalar.activation(out=one_half[:], in_=zero[:], func=ACT.Sigmoid)
+
+        def load(name, src, first, width):
+            tile = sb.tile([P, PACK, width], F32, name="raw_" + name, align_bytes=64)
+            rows = src.rearrange("g (p j) c -> (g p) j c", j=PACK)
+            nc.sync.dma_start(out=tile[:], in_=rows[:, :, first : first + width])
+            return tile[:]
 
         raw = {}
-        raw["w3"] = load("w3", w3, 0, M)
-        raw["x0"] = load("x0", x, 0, HALF)
-        raw["w1"] = load("w1", w1, 0, M)
         raw["w2"] = load("w2", w2, 0, M)
-        raw["x1"] = load("x1", x, HALF, HALF)
+        x_whole = load("x", x, 0, N)
+        raw["x0"], raw["x1"] = x_whole[:, :, 0:HALF], x_whole[:, :, HALF:N]
+        for a, vector in enumerate((th, og)):
+            nc.sync.dma_start(
+                out=vec_rows[0:P:QUAD, G * a : G * (a + 1), :],
+                in_=vector.rearrange("g (q r) o -> q g (r o)", r=QUAD),
+            )
+        raw["w1"] = load("w1", w1, 0, M)
+        raw["w3"] = load("w3", w3, 0, M)
         raw["wo"] = load("wo", wo, 0, M)
         raw["dy0"] = load("dy0", dy, 0, HALF)
         raw["dy1"] = load("dy1", dy, HALF, HALF)
         base_sb = sb.tile([P, G, N], F32, name="base_sb")
         nc.sync.dma_start(out=base_sb[:], in_=base.rearrange("g m n -> m g n"))
 
-        th_sb = sb.tile([P, G, 8], F32, name="th_sb")
-        og_sb = sb.tile([P, G, 8], F32, name="og_sb")
-        with nc.allow_non_contiguous_dma(reason="one value a partition"):
-            nc.gpsimd.dma_start(out=th_sb[:, :, 0:1], in_=th.rearrange("g m o -> m g o"))
-            nc.gpsimd.dma_start(out=og_sb[:, :, 0:1], in_=og.rearrange("g m o -> m g o"))
-        bias3 = sb.tile([P, G, 8], F32, name="bias3")
-        nc.gpsimd.tensor_scalar(out=bias3[:, :, 0:1], in0=th_sb[:, :, 0:1], scalar1=-0.5, scalar2=0.0, op0=ALU.mult, op1=ALU.add)
-
-        words = {}
+        grouped, codes, scales = {}, {}, {}
         for name in raw:
-            words[name] = sb.tile([P, raw[name].shape[2], PACK], BF16, name="bf_" + name, align_bytes=64)
-
-        def interleave(copy, name, c0, c1):
-            copy(
-                out=words[name][:, c0:c1, :].rearrange("p (c i) j -> p c j i", i=RUN),
-                in_=raw[name][:, :, c0:c1].rearrange("p j (c i) -> p c j i", i=RUN),
-            )
-
-        codes, scales = {}, {}
-
-        def quantize(name):
             width = raw[name].shape[2]
+            grouped[name] = sb.tile([P, width, PACK], BF16, name="bf_" + name, align_bytes=64)
             codes[name] = sb.tile([P, width], U32, name="codes_" + name, align_bytes=64)
             scales[name] = sb.tile([P, width], U8, name="scales_" + name, align_bytes=64)
+
+        def interleave(copy, name, first, last):
+            copy(
+                out=grouped[name][:, first:last, :].rearrange("p (c i) j -> p c j i", i=RUN),
+                in_=raw[name][:, :, first:last].rearrange("p j (c i) -> p c j i", i=RUN),
+            )
+
+        def quantize(name):
             nc.vector.quantize_mx(
                 out=codes[name][:].bitcast(FP8X4),
                 scales=scales[name][:],
-                in_=words[name][:].rearrange("p c j -> p (c j)"),
+                in_=grouped[name][:].rearrange("p c j -> p (c j)"),
             )
 
         banks = {}
@@ -80,115 +87,150 @@ def tile_rows_gptwogates_kernel(tc, x, w1, w2, w3, th, wo, dy, og, base, out):
                 banks[z, g] = ps.tile([M, N], F32, name="%s_%d" % (z, g))
 
         def product(z, weight, moving, h):
-            for c in range(0, HALF, NMM):
+            operand = moving + str(h)
+            for c in range(0, HALF, N_MM):
                 for g in range(G):
                     rows = slice(ROWS * g, ROWS * (g + 1))
                     nc.tensor.matmul_mx(
-                        out=banks[z, g][:, h * HALF + c : h * HALF + c + NMM],
+                        out=banks[z, g][:, h * HALF + c : h * HALF + c + N_MM],
                         lhsT=codes[weight][rows, :].bitcast(FP8X4),
                         lhsT_scale=scales[weight][rows, :],
-                        rhs=codes[moving][rows, c : c + NMM].bitcast(FP8X4),
-                        rhs_scale=scales[moving][rows, c : c + NMM],
+                        rhs=codes[operand][rows, c : c + N_MM].bitcast(FP8X4),
+                        rhs_scale=scales[operand][rows, c : c + N_MM],
                         start=True,
                         stop=True,
                     )
 
+        def sums(z, h, g):
+            return banks[z, g][:, h * HALF : (h + 1) * HALF]
+
+        vec_cols = sb.tile([P, 2 * G, QUAD], F32, name="vec_cols", align_bytes=64)
+        minus_th = sb.tile([P, G, 1], F32, name="minus_th")
+        gain = sb.tile([P, G, 1], F32, name="gain")
+
+        def feature_constants():
+            nc.vector.transpose(
+                out=vec_cols[:].rearrange("p a r -> p (a r)"), in_=vec_rows[:].rearrange("p a r -> p (a r)")
+            )
+            nc.vector.tensor_scalar(
+                out=minus_th[:], in0=vec_cols[:, 0:G, 0:1], scalar1=-1.0, scalar2=None, op0=ALU.mult
+            )
+            nc.vector.scalar_tensor_tensor(
+                out=gain[:], in0=vec_cols[:, G : 2 * G, 0:1], scalar=-0.25, in1=one_half[:], op0=ALU.mult, op1=ALU.mult
+            )
+
         work = {}
-        for name in ("t3", "t2", "t2sq", "p", "v", "w", "wsq", "m", "y"):
+        for name in ("t", "t_sq", "g3", "f1", "f2", "f3", "f3_sq", "odd", "y"):
             for h in range(2):
                 work[name, h] = sb.tile([P, G, HALF], F32, name="%s_%d" % (name, h))
 
-        def psum(z, g, h):
-            return banks[z, g][:, h * HALF : (h + 1) * HALF]
+        def tanh_z2(h, g):
+            nc.scalar.activation(out=work["t", h][:, g, :], in_=sums("z2", h, g), func=ACT.Tanh, scale=0.5)
 
-        def tanh3(h, g):
-            nc.scalar.activation(out=work["t3", h][:, g, :], in_=psum("z3", g, h), func=ACT.Tanh, bias=bias3[:, g, 0:1], scale=0.5)
+        def square_t(h, g):
+            nc.scalar.activation(out=work["t_sq", h][:, g, :], in_=work["t", h][:, g, :], func=ACT.Square)
 
-        def tanh2(h, g):
-            nc.scalar.activation(out=work["t2", h][:, g, :], in_=psum("z2", g, h), func=ACT.Tanh, scale=0.5)
+        def gate_z3(h, g):
+            nc.scalar.activation(
+                out=work["g3", h][:, g, :], in_=sums("z3", h, g), func=ACT.Sigmoid, bias=minus_th[:, g, :]
+            )
 
-        def sq2(h):
-            nc.scalar.activation(out=work["t2sq", h][:], in_=work["t2", h][:], func=ACT.Square)
+        def times_z1(h, g):
+            nc.vector.scalar_tensor_tensor(
+                out=work["f1", h][:, g, :], in0=work["t_sq", h][:, g, :], scalar=1.0, in1=sums("z1", h, g),
+                op0=ALU.subtract, op1=ALU.mult,
+            )
 
-        def step_p(h, g):
-            nc.vector.scalar_tensor_tensor(out=work["p", h][:, g, :], in0=work["t3", h][:, g, :], scalar=1.0, in1=psum("z1", g, h), op0=ALU.add, op1=ALU.mult)
+        def times_g3(h, groups):
+            nc.vector.tensor_tensor(
+                out=work["f2", h][:, groups, :], in0=work["f1", h][:, groups, :], in1=work["g3", h][:, groups, :],
+                op=ALU.mult,
+            )
 
-        def step_v(h):
-            nc.vector.scalar_tensor_tensor(out=work["v", h][:], in0=work["t2sq", h][:], scalar=1.0, in1=work["p", h][:], op0=ALU.subtract, op1=ALU.mult)
+        def times_c0(h, g):
+            nc.vector.tensor_tensor(
+                out=work["f3", h][:, g, :], in0=work["f2", h][:, g, :], in1=sums("c0", h, g), op=ALU.mult
+            )
 
-        def step_w(h, g):
-            nc.vector.tensor_tensor(out=work["w", h][:, g, :], in0=work["v", h][:, g, :], in1=psum("c0", g, h), op=ALU.mult)
+        def square_f3(h, g):
+            nc.scalar.activation(out=work["f3_sq", h][:, g, :], in_=work["f3", h][:, g, :], func=ACT.Square)
 
-        def sqw(h, gs):
-            nc.scalar.activation(out=work["wsq", h][:, gs, :], in_=work["w", h][:, gs, :], func=ACT.Square)
+        def times_t(h, g):
+            nc.vector.tensor_tensor(
+                out=work["odd", h][:, g, :], in0=work["f3_sq", h][:, g, :], in1=work["t", h][:, g, :], op=ALU.mult
+            )
 
-        def step_m(h, gs):
-            nc.vector.scalar_tensor_tensor(out=work["m", h][:, gs, :], in0=work["wsq", h][:, gs, :], scalar=-1.0 / 32.0, in1=work["t2", h][:, gs, :], op0=ALU.mult, op1=ALU.mult)
+        def add_base(h, g):
+            nc.vector.scalar_tensor_tensor(
+                out=work["y", h][:, g, :], in0=work["odd", h][:, g, :], scalar=gain[:, g, :],
+                in1=base_sb[:, g, h * HALF : (h + 1) * HALF], op0=ALU.mult, op1=ALU.add,
+            )
 
-        def step_y(h, g):
-            nc.vector.scalar_tensor_tensor(out=work["y", h][:, g, :], in0=work["m", h][:, g, :], scalar=og_sb[:, g, 0:1], in1=base_sb[:, g, h * HALF : (h + 1) * HALF], op0=ALU.mult, op1=ALU.add)
+        def store(h, groups):
+            nc.sync.dma_start(
+                out=out.rearrange("g m n -> m g n")[:, groups, h * HALF : (h + 1) * HALF],
+                in_=work["y", h][:, groups, :],
+            )
 
-        def store(h, gs):
-            nc.sync.dma_start(out=out.rearrange("g m n -> m g n")[:, gs, h * HALF : (h + 1) * HALF], in_=work["y", h][:, gs, :])
+        def each_group(step, h):
+            for g in range(G):
+                step(h, g)
 
-        vec, act = nc.vector.tensor_copy, nc.scalar.copy
+        on_vector, on_scalar = nc.vector.tensor_copy, nc.scalar.copy
         both = slice(0, G)
-        with tc.manual_schedule():
-            interleave(vec, "w3", 0, M)
-            quantize("w3")
-            interleave(vec, "x0", 0, 160)
-            interleave(act, "x0", 160, HALF)
-            quantize("x0")
-            product("z3", "w3", "x0", 0)
-            interleave(act, "w1", 0, M)
-            interleave(vec, "w2", 0, M)
-            quantize("w1")
-            product("z1", "w1", "x0", 0)
-            quantize("w2")
-            product("z2", "w2", "x0", 0)
-            tanh3(0, 0)
-            tanh3(0, 1)
-            step_p(0, 0)
-            interleave(vec, "x1", 0, HALF)
-            step_p(0, 1)
-            tanh2(0, 0)
-            tanh2(0, 1)
-            quantize("x1")
-            product("z3", "w3", "x1", 1)
-            product("z2", "w2", "x1", 1)
-            product("z1", "w1", "x1", 1)
-            interleave(act, "wo", 0, M)
-            sq2(0)
-            quantize("wo")
-            interleave(vec, "dy0", 0, HALF)
-            step_v(0)
-            quantize("dy0")
-            product("c0", "wo", "dy0", 0)
-            tanh3(1, 0)
-            tanh3(1, 1)
-            tanh2(1, 0)
-            tanh2(1, 1)
-            step_p(1, 0)
-            step_p(1, 1)
-            interleave(act, "dy1", 0, HALF)
-            step_w(0, 0)
-            step_w(0, 1)
-            quantize("dy1")
-            product("c0", "wo", "dy1", 1)
-            sq2(1)
-            sqw(0, both)
-            step_v(1)
-            step_m(0, both)
-            step_w(1, 0)
-            step_w(1, 1)
-            sqw(1, slice(0, 1))
-            sqw(1, slice(1, 2))
-            step_y(0, 0)
-            step_y(0, 1)
-            store(0, both)
-            step_m(1, slice(0, 1))
-            step_m(1, slice(1, 2))
-            step_y(1, 0)
-            store(1, slice(0, 1))
-            step_y(1, 1)
-            store(1, slice(1, 2))
+
+        interleave(on_vector, "w2", 0, M)
+        quantize("w2")
+        interleave(on_vector, "x0", 0, X0_VECTOR)
+        interleave(on_scalar, "x0", X0_VECTOR, HALF)
+        interleave(on_vector, "x1", 0, X1_VECTOR)
+        interleave(on_scalar, "x1", X1_VECTOR, HALF)
+        quantize("x0")
+        product("z2", "w2", "x", 0)
+        interleave(on_vector, "w1", 0, M)
+        quantize("x1")
+        interleave(on_scalar, "w3", 0, M)
+        quantize("w1")
+        product("z1", "w1", "x", 0)
+
+        each_group(tanh_z2, 0)
+        product("z2", "w2", "x", 1)
+        interleave(on_vector, "wo", 0, M)
+        quantize("w3")
+        product("z3", "w3", "x", 0)
+        each_group(square_t, 0)
+        quantize("wo")
+        feature_constants()
+        times_z1(0, 0)
+        interleave(on_vector, "dy0", 0, HALF)
+        times_z1(0, 1)
+        product("z1", "w1", "x", 1)
+
+        each_group(tanh_z2, 1)
+        each_group(gate_z3, 0)
+        quantize("dy0")
+        product("c0", "wo", "dy", 0)
+        product("z3", "w3", "x", 1)
+        each_group(square_t, 1)
+        times_g3(0, both)
+        each_group(times_z1, 1)
+        interleave(on_scalar, "dy1", 0, HALF)
+        each_group(times_c0, 0)
+
+        for g in range(G):
+            gate_z3(1, g)
+            square_f3(0, g)
+        quantize("dy1")
+        product("c0", "wo", "dy", 1)
+        for g in range(G):
+            times_g3(1, slice(g, g + 1))
+            times_t(0, g)
+        each_group(times_c0, 1)
+        each_group(square_f3, 1)
+
+        each_group(add_base, 0)
+        store(0, both)
+        each_group(times_t, 1)
+        for g in range(G):
+            add_base(1, g)
+            store(1, slice(g, g + 1))

from contextlib import ExitStack

import concourse.mybir as mybir

G, D, M, N = 2, 256, 128, 512
FLOPS = 4 * 2 * G * D * M * N

F32 = mybir.dt.float32
BF16 = mybir.dt.bfloat16
U32 = mybir.dt.uint32
U8 = mybir.dt.uint8
FP8X4 = mybir.dt.float8_e4m3fn_x4
ACT = mybir.ActivationFunctionType
ALU = mybir.AluOpType

P = 128
PACK = 4
ROWS = D // PACK
HALF = N // 2
N_MM = 128
RUN = 4
QUAD = 32
X0_VECTOR = 168
X1_VECTOR = 128


def tile_rows_gptwogates_kernel(tc, x, w1, w2, w3, th, wo, dy, og, base, out):
    nc = tc.nc
    with ExitStack() as ctx:
        sb = ctx.enter_context(tc.tile_pool(name="sb", bufs=1))
        ps = ctx.enter_context(tc.psum_pool(name="ps", bufs=1))
        ctx.enter_context(tc.manual_schedule())

        vec_rows = sb.tile([P, 2 * G, QUAD], F32, name="vec_rows", align_bytes=64)
        nc.vector.memset(vec_rows[:], 0.0)
        zero = sb.tile([P, G, 1], F32, name="zero")
        nc.vector.memset(zero[:], 0.0)
        one_half = sb.tile([P, G, 1], F32, name="one_half")
        nc.scalar.activation(out=one_half[:], in_=zero[:], func=ACT.Sigmoid)

        def load(name, src, first, width):
            tile = sb.tile([P, PACK, width], F32, name="raw_" + name, align_bytes=64)
            rows = src.rearrange("g (p j) c -> (g p) j c", j=PACK)
            nc.sync.dma_start(out=tile[:], in_=rows[:, :, first : first + width])
            return tile[:]

        raw = {}
        raw["w2"] = load("w2", w2, 0, M)
        x_whole = load("x", x, 0, N)
        raw["x0"], raw["x1"] = x_whole[:, :, 0:HALF], x_whole[:, :, HALF:N]
        for a, vector in enumerate((th, og)):
            nc.sync.dma_start(
                out=vec_rows[0:P:QUAD, G * a : G * (a + 1), :],
                in_=vector.rearrange("g (q r) o -> q g (r o)", r=QUAD),
            )
        raw["w1"] = load("w1", w1, 0, M)
        raw["w3"] = load("w3", w3, 0, M)
        raw["wo"] = load("wo", wo, 0, M)
        raw["dy0"] = load("dy0", dy, 0, HALF)
        raw["dy1"] = load("dy1", dy, HALF, HALF)
        base_sb = sb.tile([P, G, N], F32, name="base_sb")
        nc.sync.dma_start(out=base_sb[:], in_=base.rearrange("g m n -> m g n"))

        grouped, codes, scales = {}, {}, {}
        for name in raw:
            width = raw[name].shape[2]
            grouped[name] = sb.tile([P, width, PACK], BF16, name="bf_" + name, align_bytes=64)
            codes[name] = sb.tile([P, width], U32, name="codes_" + name, align_bytes=64)
            scales[name] = sb.tile([P, width], U8, name="scales_" + name, align_bytes=64)

        def interleave(copy, name, first, last):
            copy(
                out=grouped[name][:, first:last, :].rearrange("p (c i) j -> p c j i", i=RUN),
                in_=raw[name][:, :, first:last].rearrange("p j (c i) -> p c j i", i=RUN),
            )

        def quantize(name):
            nc.vector.quantize_mx(
                out=codes[name][:].bitcast(FP8X4),
                scales=scales[name][:],
                in_=grouped[name][:].rearrange("p c j -> p (c j)"),
            )

        banks = {}
        for z in ("z1", "z2", "z3", "c0"):
            for g in range(G):
                banks[z, g] = ps.tile([M, N], F32, name="%s_%d" % (z, g))

        def product(z, weight, moving, h):
            operand = moving + str(h)
            for c in range(0, HALF, N_MM):
                for g in range(G):
                    rows = slice(ROWS * g, ROWS * (g + 1))
                    nc.tensor.matmul_mx(
                        out=banks[z, g][:, h * HALF + c : h * HALF + c + N_MM],
                        lhsT=codes[weight][rows, :].bitcast(FP8X4),
                        lhsT_scale=scales[weight][rows, :],
                        rhs=codes[operand][rows, c : c + N_MM].bitcast(FP8X4),
                        rhs_scale=scales[operand][rows, c : c + N_MM],
                        start=True,
                        stop=True,
                    )

        def sums(z, h, g):
            return banks[z, g][:, h * HALF : (h + 1) * HALF]

        vec_cols = sb.tile([P, 2 * G, QUAD], F32, name="vec_cols", align_bytes=64)
        minus_th = sb.tile([P, G, 1], F32, name="minus_th")
        gain = sb.tile([P, G, 1], F32, name="gain")

        def feature_constants():
            nc.vector.transpose(
                out=vec_cols[:].rearrange("p a r -> p (a r)"), in_=vec_rows[:].rearrange("p a r -> p (a r)")
            )
            nc.vector.tensor_scalar(
                out=minus_th[:], in0=vec_cols[:, 0:G, 0:1], scalar1=-1.0, scalar2=None, op0=ALU.mult
            )
            nc.vector.scalar_tensor_tensor(
                out=gain[:], in0=vec_cols[:, G : 2 * G, 0:1], scalar=-0.25, in1=one_half[:], op0=ALU.mult, op1=ALU.mult
            )

        work = {}
        for name in ("t", "t_sq", "g3", "f1", "f2", "f3", "f3_sq", "odd", "y"):
            for h in range(2):
                work[name, h] = sb.tile([P, G, HALF], F32, name="%s_%d" % (name, h))

        def tanh_z2(h, g):
            nc.scalar.activation(out=work["t", h][:, g, :], in_=sums("z2", h, g), func=ACT.Tanh, scale=0.5)

        def square_t(h, g):
            nc.scalar.activation(out=work["t_sq", h][:, g, :], in_=work["t", h][:, g, :], func=ACT.Square)

        def gate_z3(h, g):
            nc.scalar.activation(
                out=work["g3", h][:, g, :], in_=sums("z3", h, g), func=ACT.Sigmoid, bias=minus_th[:, g, :]
            )

        def times_z1(h, g):
            nc.vector.scalar_tensor_tensor(
                out=work["f1", h][:, g, :], in0=work["t_sq", h][:, g, :], scalar=1.0, in1=sums("z1", h, g),
                op0=ALU.subtract, op1=ALU.mult,
            )

        def times_g3(h, groups):
            nc.vector.tensor_tensor(
                out=work["f2", h][:, groups, :], in0=work["f1", h][:, groups, :], in1=work["g3", h][:, groups, :],
                op=ALU.mult,
            )

        def times_c0(h, g):
            nc.vector.tensor_tensor(
                out=work["f3", h][:, g, :], in0=work["f2", h][:, g, :], in1=sums("c0", h, g), op=ALU.mult
            )

        def square_f3(h, g):
            nc.scalar.activation(out=work["f3_sq", h][:, g, :], in_=work["f3", h][:, g, :], func=ACT.Square)

        def times_t(h, g):
            nc.vector.tensor_tensor(
                out=work["odd", h][:, g, :], in0=work["f3_sq", h][:, g, :], in1=work["t", h][:, g, :], op=ALU.mult
            )

        def add_base(h, g):
            nc.vector.scalar_tensor_tensor(
                out=work["y", h][:, g, :], in0=work["odd", h][:, g, :], scalar=gain[:, g, :],
                in1=base_sb[:, g, h * HALF : (h + 1) * HALF], op0=ALU.mult, op1=ALU.add,
            )

        def store(h, groups):
            nc.sync.dma_start(
                out=out.rearrange("g m n -> m g n")[:, groups, h * HALF : (h + 1) * HALF],
                in_=work["y", h][:, groups, :],
            )

        def each_group(step, h):
            for g in range(G):
                step(h, g)

        on_vector, on_scalar = nc.vector.tensor_copy, nc.scalar.copy
        both = slice(0, G)

        interleave(on_vector, "w2", 0, M)
        quantize("w2")
        interleave(on_vector, "x0", 0, X0_VECTOR)
        interleave(on_scalar, "x0", X0_VECTOR, HALF)
        interleave(on_vector, "x1", 0, X1_VECTOR)
        interleave(on_scalar, "x1", X1_VECTOR, HALF)
        quantize("x0")
        product("z2", "w2", "x", 0)
        interleave(on_vector, "w1", 0, M)
        quantize("x1")
        interleave(on_scalar, "w3", 0, M)
        quantize("w1")
        product("z1", "w1", "x", 0)

        each_group(tanh_z2, 0)
        product("z2", "w2", "x", 1)
        interleave(on_vector, "wo", 0, M)
        quantize("w3")
        product("z3", "w3", "x", 0)
        each_group(square_t, 0)
        quantize("wo")
        feature_constants()
        times_z1(0, 0)
        interleave(on_vector, "dy0", 0, HALF)
        times_z1(0, 1)
        product("z1", "w1", "x", 1)

        each_group(tanh_z2, 1)
        each_group(gate_z3, 0)
        quantize("dy0")
        product("c0", "wo", "dy", 0)
        product("z3", "w3", "x", 1)
        each_group(square_t, 1)
        times_g3(0, both)
        each_group(times_z1, 1)
        interleave(on_scalar, "dy1", 0, HALF)
        each_group(times_c0, 0)

        for g in range(G):
            gate_z3(1, g)
            square_f3(0, g)
        quantize("dy1")
        product("c0", "wo", "dy", 1)
        for g in range(G):
            times_g3(1, slice(g, g + 1))
            times_t(0, g)
        each_group(times_c0, 1)
        each_group(square_f3, 1)

        each_group(add_base, 0)
        store(0, both)
        each_group(times_t, 1)
        for g in range(G):
            add_base(1, g)
            store(1, slice(g, g + 1))
